import numpy as np
import ml_dtypes


def mxq(x, axis, fmt="e4m3"):
    dtype, down = {"e4m3": (ml_dtypes.float8_e4m3fn, 7), "e5m2": (ml_dtypes.float8_e5m2, 14)}[fmt]
    v = np.moveaxis(np.asarray(x, np.float32).astype(ml_dtypes.bfloat16).astype(np.float64), axis, -1)
    blocks = v.reshape(v.shape[:-1] + (-1, 32))
    amax = np.abs(blocks).max(-1, keepdims=True)
    byte = np.maximum(np.where(amax > 0, np.frexp(amax)[1] - 1 + 127, 0) - down, 1)
    scale = np.exp2(byte - 127.0)
    codes = (blocks / scale).astype(np.float32).astype(dtype).astype(np.float64)
    return np.moveaxis((codes * scale).reshape(v.shape), -1, axis)


WIDE = False


def mx_kscale(k):
    if not WIDE:
        return np.ones(k)
    levels = np.array([10, -10, 5, -5, 0])
    if k % 512:
        return np.exp2(np.random.permutation(np.resize(levels, k // 32))).repeat(32)
    a = np.empty((k // 512, 16))
    for p in range(k // 512):
        a[p, :8] = np.random.permutation(np.resize(levels, 8))
        for g in range(8):
            far = levels[np.abs(levels - a[p, g]) >= 10]
            a[p, g + 8] = far[np.random.randint(len(far))]
    return np.exp2(a.ravel()).repeat(32)


def f64(x):
    return np.asarray(x).astype(np.float64)


def striped(idx):
    return np.tile(np.asarray(idx).reshape(-1, 16).T, (8, 1)).astype(np.uint16)


def unstriped(offs):
    return offs[:16].T.reshape(-1).astype(np.int64)


E2M1 = np.array([0.0, 0.5, 1.0, 1.5, 2.0, 3.0, 4.0, 6.0, -0.0, -0.5, -1.0, -1.5, -2.0, -3.0, -4.0, -6.0])


def pack_weight(w, fmt):
    k, n = w.shape
    w = f64(np.asarray(w, np.float32).astype(ml_dtypes.bfloat16)).reshape(k // 32, 32, n)
    amax = np.abs(w).max(1)
    if fmt == "e4m3":
        byte = np.frexp(amax)[1] - 1 + 127 - 7
    else:
        mant, ex = np.frexp(amax / 6.0)
        byte = np.where(mant > 0.5, ex, ex - 1) + 127
    byte = np.clip(np.where(amax > 0, byte, 1), 1, 254)
    scaled = (w * np.exp2(127.0 - byte)[:, None, :]).reshape(k, n).astype(np.float32)
    by_word = np.ascontiguousarray(scaled.reshape(k // 512, 128, 4, n).transpose(0, 1, 3, 2))
    if fmt == "e4m3":
        words = by_word.astype(ml_dtypes.float8_e4m3fn).view(np.uint8)
    else:
        c = by_word.astype(ml_dtypes.float4_e2m1fn).view(np.uint8) & 0xF
        words = (c[..., 0::2] | (c[..., 1::2] << 4)).reshape(k // 512, 128, 2 * n)
    return np.ascontiguousarray(words), np.ascontiguousarray(byte.astype(np.uint8).reshape(k // 512, 16, n))


def unpack_weight(words, scales, fmt):
    g, _, n = scales.shape
    words = np.ascontiguousarray(words).reshape(g, 128, n, -1)
    if fmt == "e4m3":
        vals = words.view(ml_dtypes.float8_e4m3fn).astype(np.float64)
    else:
        nib = np.empty((g, 128, n, 4), np.uint8)
        nib[..., 0::2] = words & 0xF
        nib[..., 1::2] = words >> 4
        vals = E2M1[nib]
    vals = vals * np.repeat(np.exp2(scales.astype(np.float64) - 127.0), 8, axis=1)[..., None]
    return vals.transpose(0, 1, 3, 2).reshape(g * 512, n)


D, T, I, Q, J, U, M = 512, 2048, 512, 128, 512, 1024, 2048


def setup_inputs():
    n = np.random.standard_normal
    idx = np.random.permutation(T)[:I]
    idx2 = np.random.permutation(U)[:J]
    idx3 = np.random.permutation(M)[:I]
    fd = mx_kscale(D)
    fj = mx_kscale(J)
    tiesp = pack_weight(n((J, T)) * 0.08 / fj[:, None], "e4m3")
    return {
        "query": (n((D, Q)) * 1.0 / np.sqrt(D) * fd[:, None]).astype(np.float32),
        "hubs": (n((D, U)) / fd[:, None]).astype(np.float32),
        "hf": (np.random.uniform(0.5, 2.0, (J, 1)) * fj[:, None]).astype(np.float32),
        "ties_words": tiesp[0],
        "ties_scales": tiesp[1],
        "level": (np.random.uniform(0.05, 0.2, (Q, 1))).astype(np.float32),
        "old": (np.random.uniform(0.0, 2.0, (Q, M))).astype(np.float32),
        "fade": (np.random.uniform(0.3, 0.9, (Q, 1))).astype(np.float32),
        "offs": striped(idx),
        "offs2": striped(idx2),
        "offs3": striped(idx3),
    }


def reference(query, hubs, hf, ties_words, ties_scales, level, old, fade, offs, offs2, offs3):
    idx = unstriped(offs)
    idx2 = unstriped(offs2)
    idx3 = unstriped(offs3)
    tiesu = unpack_weight(ties_words, ties_scales, "e4m3")
    hubsidx2q = mxq(f64(hubs)[:, idx2], 0, "e4m3")
    queryq = mxq(f64(query), 0, "e4m3")
    hb = hubsidx2q.T @ queryq
    hp = np.maximum(hb, 0.0) * f64(hf)
    hpq = mxq(hp, 0, "e4m3")
    tiesidxg = tiesu[:, idx]
    s = hpq.T @ tiesidxg
    p = np.exp(s - np.max(s, axis=1, keepdims=True))
    r = p / np.sum(p, axis=1, keepdims=True)
    w = np.maximum(r - np.max(r, axis=1, keepdims=True) * f64(level), 0.0)
    ws = w * 256.0
    wf = np.zeros((Q, M))
    wf[:, idx3] = ws
    y = f64(old) * f64(fade) + wf
    return y

@@ -1,0 +1,156 @@
+from contextlib import ExitStack
+
+import concourse.mybir as mybir
+
+D, T, I, Q, J, U, M = 512, 2048, 512, 128, 512, 1024, 2048
+FLOPS = 2 * D * J * Q + 2 * J * Q * I
+
+F32 = mybir.dt.float32
+BF16 = mybir.dt.bfloat16
+I32 = mybir.dt.int32
+U32 = mybir.dt.uint32
+U16 = mybir.dt.uint16
+U8 = mybir.dt.uint8
+FP8X4 = mybir.dt.float8_e4m3fn_x4
+ALU = mybir.AluOpType
+ACT = mybir.ActivationFunctionType
+AX = mybir.AxisListType
+
+P = 128
+PACK = 4
+LIST_COLS = 32
+OUT_CHUNKS = (256, 512, 512, 512, 256)
+
+
+def tile_attend_relayed_excess_counts_kernel(
+    tc, query, hubs, hf, ties_words, ties_scales, level, old, fade, offs, offs2, offs3, out
+):
+    nc = tc.nc
+    with ExitStack() as ctx:
+        sb = ctx.enter_context(tc.tile_pool(name="sb", bufs=1))
+        ps = ctx.enter_context(tc.psum_pool(name="ps", bufs=1))
+
+        tok_list = sb.tile([P, LIST_COLS], U16, name="tok_list")
+        hub_list = sb.tile([P, LIST_COLS], U16, name="hub_list")
+        col_list = sb.tile([P, LIST_COLS], U16, name="col_list")
+        hub_rows = [sb.tile([P, U], F32, name="hub_rows%d" % t) for t in range(PACK)]
+        q_raw = sb.tile([P, PACK, Q], F32, name="q_raw")
+        tie_words = sb.tile([P, T], I32, name="tie_words")
+        tie_bytes = sb.tile([P, T], U8, name="tie_bytes")
+        old_sb = sb.tile([P, M], F32, name="old_sb")
+        hf_sb = sb.tile([P, PACK], F32, name="hf_sb")
+        level_sb = sb.tile([P, 1], F32, name="level_sb")
+        fade_sb = sb.tile([P, 1], F32, name="fade_sb")
+        placed = sb.tile([P, M], F32, name="placed")
+
+        nc.vector.memset(tie_bytes[:].bitcast(I32), 0)
+        nc.vector.memset(placed[:], 0.0)
+
+        hubs_v = hubs.rearrange("(p t) u -> p t u", t=PACK)
+        nc.sync.dma_start(hub_list[:], offs2)
+        nc.sync.dma_start(hub_rows[0][:], hubs_v[:, 0, :])
+        nc.sync.dma_start(q_raw[:], query.rearrange("(p t) q -> p t q", t=PACK))
+        for t in range(1, PACK):
+            nc.sync.dma_start(hub_rows[t][:], hubs_v[:, t, :])
+        nc.sync.dma_start(tok_list[:], offs)
+        nc.sync.dma_start(tie_words[:], ties_words[0].rearrange("p n t -> p (n t)").bitcast(I32))
+        nc.sync.dma_start(old_sb[:], old)
+        nc.sync.dma_start(col_list[:], offs3)
+        for g in range(4):
+            nc.gpsimd.dma_start(
+                tie_bytes[32 * g : 32 * g + 4, :].bitcast(I32),
+                ties_scales[0, 4 * g : 4 * g + 4, :].bitcast(I32),
+            )
+        nc.gpsimd.dma_start(hf_sb[:], hf.rearrange("(p r) o -> p (r o)", r=PACK))
+        nc.gpsimd.dma_start(level_sb[:], level)
+        nc.gpsimd.dma_start(fade_sb[:], fade)
+
+        picked = sb.tile([P, PACK, J], BF16, name="picked")
+        half = J // 2
+        hc = LIST_COLS // 2
+        nc.scalar.activation(picked[:, 0, :], hub_rows[0][:].indirect(hub_list[:]), ACT.Copy)
+
+        q_bf = sb.tile([P, Q, PACK], BF16, name="q_bf", align_bytes=64)
+        q_codes = sb.tile([P, Q], U32, name="q_codes", align_bytes=64)
+        q_scales = sb.tile([P, Q], U8, name="q_scales", align_bytes=64)
+        nc.vector.tensor_copy(q_bf[:], q_raw[:].rearrange("p t q -> p q t"))
+        nc.vector.quantize_mx(q_codes[:].bitcast(FP8X4), q_scales[:], q_bf[:].rearrange("p q t -> p (q t)"))
+
+        nc.vector.tensor_copy(picked[:, 1, :], hub_rows[1][:].indirect(hub_list[:]))
+        got_bytes = sb.tile([P, I], U8, name="got_bytes", align_bytes=64)
+        nc.vector.tensor_copy(got_bytes[:], tie_bytes[:].indirect(tok_list[:]))
+        nc.scalar.activation(picked[:, 2, :], hub_rows[2][:].indirect(hub_list[:]), ACT.Copy)
+        nc.vector.tensor_copy(picked[:, 3, 0:half], hub_rows[3][:].indirect(hub_list[:, 0:hc]))
+        nc.scalar.activation(picked[:, 3, half:J], hub_rows[3][:].indirect(hub_list[:, hc:LIST_COLS]), ACT.Copy)
+
+        src = picked[:].rearrange("p t (s r) -> p r s t", r=PACK)
+        hub_bf = [sb.tile([P, 2, P, PACK], BF16, name="hub_bf%d" % h, align_bytes=64) for h in range(2)]
+        hub_codes = [sb.tile([P, 2 * P], U32, name="hub_codes%d" % h, align_bytes=64) for h in range(2)]
+        hub_scales = [sb.tile([P, 2 * P], U8, name="hub_scales%d" % h, align_bytes=64) for h in range(2)]
+        nc.vector.tensor_copy(hub_bf[0][:], src[:, 0:2])
+        nc.scalar.copy(hub_bf[1][:, 1], src[:, 3])
+        nc.vector.tensor_copy(hub_bf[1][:, 0], src[:, 2])
+        hb = ps.tile([P, PACK, Q], F32, name="hb")
+        for h in range(2):
+            nc.vector.quantize_mx(
+                hub_codes[h][:].bitcast(FP8X4), hub_scales[h][:], hub_bf[h][:].rearrange("p r s t -> p (r s t)")
+            )
+            for e in range(2):
+                cols = slice(e * P, (e + 1) * P)
+                nc.tensor.matmul_mx(
+                    hb[:, 2 * h + e, :],
+                    lhsT=hub_codes[h][:, cols].bitcast(FP8X4),
+                    lhsT_scale=hub_scales[h][:, cols],
+                    rhs=q_codes[:].bitcast(FP8X4),
+                    rhs_scale=q_scales[:],
+                    start=True,
+                    stop=True,
+                )
+
+        got_words = sb.tile([P, I], U32, name="got_words", align_bytes=64)
+        nc.vector.tensor_copy(got_words[:], tie_words[:].bitcast(U32).indirect(tok_list[:]))
+
+        hp_bf = sb.tile([P, Q, PACK], BF16, name="hp_bf", align_bytes=64)
+        nc.vector.scalar_tensor_tensor(
+            hp_bf[:],
+            hb[:].rearrange("p r q -> p q r"),
+            0.0,
+            hf_sb[:].unsqueeze(1).to_broadcast([P, Q, PACK]),
+            ALU.max,
+            ALU.mult,
+        )
+        hp_codes = sb.tile([P, Q], U32, name="hp_codes", align_bytes=64)
+        hp_scales = sb.tile([P, Q], U8, name="hp_scales", align_bytes=64)
+        nc.vector.quantize_mx(hp_codes[:].bitcast(FP8X4), hp_scales[:], hp_bf[:].rearrange("p q r -> p (q r)"))
+
+        scores = ps.tile([P, I], F32, name="scores")
+        nc.tensor.matmul_mx(
+            scores[:],
+            lhsT=hp_codes[:].bitcast(FP8X4),
+            lhsT_scale=hp_scales[:],
+            rhs=got_words[:].bitcast(FP8X4),
+            rhs_scale=got_bytes[:],
+            start=True,
+            stop=True,
+        )
+
+        neg_max = sb.tile([P, 1], F32, name="neg_max")
+        nc.vector.tensor_reduce(neg_max[:], scores[:], AX.X, ALU.max, negate=True)
+        p_sb = sb.tile([P, I], F32, name="p_sb")
+        row_sum = sb.tile([P, 1], F32, name="row_sum")
+        nc.scalar.activation(p_sb[:], scores[:], ACT.Exp, bias=neg_max[:], accum_out=row_sum[:])
+        inv_sum = sb.tile([P, 1], F32, name="inv_sum")
+        nc.vector.reciprocal(inv_sum[:], row_sum[:])
+        excess = sb.tile([P, I], F32, name="excess")
+        nc.vector.tensor_scalar(excess[:], p_sb[:], level_sb[:], 0.0, ALU.subtract, ALU.max)
+        ws = sb.tile([P, I], F32, name="ws")
+        nc.vector.tensor_scalar(ws[:], excess[:], inv_sum[:], 256.0, ALU.mult, ALU.mult)
+        nc.vector.tensor_copy(placed[:].indirect(col_list[:]), ws[:])
+
+        c0 = 0
+        for k, width in enumerate(OUT_CHUNKS):
+            cols = slice(c0, c0 + width)
+            res = sb.tile([P, width], F32, name="res%d" % k)
+            nc.vector.scalar_tensor_tensor(res[:], old_sb[:, cols], fade_sb[:], placed[:, cols], ALU.mult, ALU.add)
+            nc.sync.dma_start(out[:, cols], res[:])
+            c0 = c0 + width

@@ -19,6 +19,7 @@ AX = mybir.AxisListType
 P = 128
 PACK = 4
 LIST_COLS = 32
+N_EARLY = 256
 OUT_CHUNKS = (256, 512, 512, 512, 256)
 
 
@@ -43,72 +44,78 @@ def tile_attend_relayed_excess_counts_kernel(
         fade_sb = sb.tile([P, 1], F32, name="fade_sb")
         placed = sb.tile([P, M], F32, name="placed")
 
-        nc.vector.memset(tie_bytes[:].bitcast(I32), 0)
-        nc.vector.memset(placed[:], 0.0)
+        nc.gpsimd.memset(tie_bytes[:].bitcast(I32), 0)
+        nc.gpsimd.dma_start(hf_sb[:], hf.rearrange("(p r) o -> p (r o)", r=PACK))
+        nc.gpsimd.memset(placed[:], 0.0)
 
+        nc.scalar.dma_start(level_sb[:], level)
+        staged = sb.tile([P, 2, T // 4], I32, name="staged")
+        scale_rows = ties_scales[0].bitcast(I32).rearrange("(h g r) c -> h r g c", h=2, g=2)
+        for h in range(2):
+            nc.scalar.dma_start(staged[64 * h : 64 * h + 4], scale_rows[h])
         hubs_v = hubs.rearrange("(p t) u -> p t u", t=PACK)
         nc.sync.dma_start(hub_list[:], offs2)
         nc.sync.dma_start(hub_rows[0][:], hubs_v[:, 0, :])
-        nc.sync.dma_start(q_raw[:], query.rearrange("(p t) q -> p t q", t=PACK))
+        nc.sync.dma_start(tok_list[:], offs)
         for t in range(1, PACK):
             nc.sync.dma_start(hub_rows[t][:], hubs_v[:, t, :])
-        nc.sync.dma_start(tok_list[:], offs)
+        nc.sync.dma_start(q_raw[:], query.rearrange("(p t) q -> p t q", t=PACK))
         nc.sync.dma_start(tie_words[:], ties_words[0].rearrange("p n t -> p (n t)").bitcast(I32))
         nc.sync.dma_start(old_sb[:], old)
         nc.sync.dma_start(col_list[:], offs3)
+        nc.sync.dma_start(fade_sb[:], fade)
+
+        floor_sb = sb.tile([P, 1], F32, name="floor_sb")
+        nc.scalar.activation(floor_sb[:], level_sb[:], ACT.Copy, scale=-256.0)
         for g in range(4):
-            nc.gpsimd.dma_start(
-                tie_bytes[32 * g : 32 * g + 4, :].bitcast(I32),
-                ties_scales[0, 4 * g : 4 * g + 4, :].bitcast(I32),
-            )
-        nc.gpsimd.dma_start(hf_sb[:], hf.rearrange("(p r) o -> p (r o)", r=PACK))
-        nc.gpsimd.dma_start(level_sb[:], level)
-        nc.gpsimd.dma_start(fade_sb[:], fade)
+            lo = 64 * (g // 2)
+            nc.vector.tensor_copy(tie_bytes[32 * g : 32 * g + 4, :].bitcast(I32), staged[lo : lo + 4, g % 2, :])
 
         picked = sb.tile([P, PACK, J], BF16, name="picked")
         half = J // 2
         hc = LIST_COLS // 2
-        nc.scalar.activation(picked[:, 0, :], hub_rows[0][:].indirect(hub_list[:]), ACT.Copy)
-
-        q_bf = sb.tile([P, Q, PACK], BF16, name="q_bf", align_bytes=64)
-        q_codes = sb.tile([P, Q], U32, name="q_codes", align_bytes=64)
-        q_scales = sb.tile([P, Q], U8, name="q_scales", align_bytes=64)
-        nc.vector.tensor_copy(q_bf[:], q_raw[:].rearrange("p t q -> p q t"))
-        nc.vector.quantize_mx(q_codes[:].bitcast(FP8X4), q_scales[:], q_bf[:].rearrange("p q t -> p (q t)"))
-
-        nc.vector.tensor_copy(picked[:, 1, :], hub_rows[1][:].indirect(hub_list[:]))
         got_bytes = sb.tile([P, I], U8, name="got_bytes", align_bytes=64)
+        nc.scalar.activation(picked[:, 0, :], hub_rows[0][:].indirect(hub_list[:]), ACT.Copy)
         nc.vector.tensor_copy(got_bytes[:], tie_bytes[:].indirect(tok_list[:]))
-        nc.scalar.activation(picked[:, 2, :], hub_rows[2][:].indirect(hub_list[:]), ACT.Copy)
-        nc.vector.tensor_copy(picked[:, 3, 0:half], hub_rows[3][:].indirect(hub_list[:, 0:hc]))
-        nc.scalar.activation(picked[:, 3, half:J], hub_rows[3][:].indirect(hub_list[:, hc:LIST_COLS]), ACT.Copy)
+        nc.scalar.activation(picked[:, 1, :], hub_rows[1][:].indirect(hub_list[:]), ACT.Copy)
+        for t in (2, 3):
+            nc.vector.tensor_copy(picked[:, t, 0:half], hub_rows[t][:].indirect(hub_list[:, 0:hc]))
+            nc.scalar.activation(picked[:, t, half:J], hub_rows[t][:].indirect(hub_list[:, hc:LIST_COLS]), ACT.Copy)
 
         src = picked[:].rearrange("p t (s r) -> p r s t", r=PACK)
-        hub_bf = [sb.tile([P, 2, P, PACK], BF16, name="hub_bf%d" % h, align_bytes=64) for h in range(2)]
-        hub_codes = [sb.tile([P, 2 * P], U32, name="hub_codes%d" % h, align_bytes=64) for h in range(2)]
-        hub_scales = [sb.tile([P, 2 * P], U8, name="hub_scales%d" % h, align_bytes=64) for h in range(2)]
-        nc.vector.tensor_copy(hub_bf[0][:], src[:, 0:2])
-        nc.scalar.copy(hub_bf[1][:, 1], src[:, 3])
-        nc.vector.tensor_copy(hub_bf[1][:, 0], src[:, 2])
+        first_bf = sb.tile([P, 3, P, PACK], BF16, name="first_bf", tag="early", align_bytes=64)
+        first_codes = sb.tile([P, 3, P], U32, name="first_codes", align_bytes=64)
+        first_scales = sb.tile([P, 3, P], U8, name="first_scales", align_bytes=64)
+        second_bf = sb.tile([P, 2, P, PACK], BF16, name="second_bf", align_bytes=64)
+        second_codes = sb.tile([P, 2, P], U32, name="second_codes", tag="late", align_bytes=64)
+        second_scales = sb.tile([P, 2, P], U8, name="second_scales", align_bytes=64)
+        nc.scalar.copy(first_bf[:, 2], q_raw[:].rearrange("p t q -> p q t"))
+        nc.vector.tensor_copy(first_bf[:, 0:2], src[:, 0:2])
+        nc.vector.tensor_copy(second_bf[:, 0], src[:, 2])
+        nc.scalar.copy(second_bf[:, 1], src[:, 3])
         hb = ps.tile([P, PACK, Q], F32, name="hb")
-        for h in range(2):
+        for h, (bf, codes, scales) in enumerate(
+            ((first_bf, first_codes, first_scales), (second_bf, second_codes, second_scales))
+        ):
             nc.vector.quantize_mx(
-                hub_codes[h][:].bitcast(FP8X4), hub_scales[h][:], hub_bf[h][:].rearrange("p r s t -> p (r s t)")
+                codes[:].rearrange("p r s -> p (r s)").bitcast(FP8X4),
+                scales[:].rearrange("p r s -> p (r s)"),
+                bf[:].rearrange("p r s t -> p (r s t)"),
             )
             for e in range(2):
-                cols = slice(e * P, (e + 1) * P)
                 nc.tensor.matmul_mx(
                     hb[:, 2 * h + e, :],
-                    lhsT=hub_codes[h][:, cols].bitcast(FP8X4),
-                    lhsT_scale=hub_scales[h][:, cols],
-                    rhs=q_codes[:].bitcast(FP8X4),
-                    rhs_scale=q_scales[:],
+                    lhsT=codes[:, e, :].bitcast(FP8X4),
+                    lhsT_scale=scales[:, e, :],
+                    rhs=first_codes[:, 2, :].bitcast(FP8X4),
+                    rhs_scale=first_scales[:, 2, :],
                     start=True,
                     stop=True,
                 )
 
-        got_words = sb.tile([P, I], U32, name="got_words", align_bytes=64)
-        nc.vector.tensor_copy(got_words[:], tie_words[:].bitcast(U32).indirect(tok_list[:]))
+        tie_window = tie_words[:].bitcast(U32)
+        words_a = sb.tile([P, N_EARLY], U32, name="words_a", tag="early", align_bytes=64)
+        nc.vector.tensor_copy(words_a[:], tie_window.indirect(tok_list[:, 0 : N_EARLY // 16]))
 
         hp_bf = sb.tile([P, Q, PACK], BF16, name="hp_bf", align_bytes=64)
         nc.vector.scalar_tensor_tensor(
@@ -119,21 +126,23 @@ def tile_attend_relayed_excess_counts_kernel(
             ALU.max,
             ALU.mult,
         )
+        words_b = sb.tile([P, I - N_EARLY], U32, name="words_b", tag="late", align_bytes=64)
+        nc.vector.tensor_copy(words_b[:], tie_window.indirect(tok_list[:, N_EARLY // 16 : LIST_COLS]))
         hp_codes = sb.tile([P, Q], U32, name="hp_codes", align_bytes=64)
         hp_scales = sb.tile([P, Q], U8, name="hp_scales", align_bytes=64)
         nc.vector.quantize_mx(hp_codes[:].bitcast(FP8X4), hp_scales[:], hp_bf[:].rearrange("p q r -> p (q r)"))
 
         scores = ps.tile([P, I], F32, name="scores")
-        nc.tensor.matmul_mx(
-            scores[:],
-            lhsT=hp_codes[:].bitcast(FP8X4),
-            lhsT_scale=hp_scales[:],
-            rhs=got_words[:].bitcast(FP8X4),
-            rhs_scale=got_bytes[:],
-            start=True,
-            stop=True,
-        )
-
+        for words, lo, hi in ((words_a, 0, N_EARLY), (words_b, N_EARLY, I)):
+            nc.tensor.matmul_mx(
+                scores[:, lo:hi],
+                lhsT=hp_codes[:].bitcast(FP8X4),
+                lhsT_scale=hp_scales[:],
+                rhs=words[:].bitcast(FP8X4),
+                rhs_scale=got_bytes[:, lo:hi],
+                start=True,
+                stop=True,
+            )
         neg_max = sb.tile([P, 1], F32, name="neg_max")
         nc.vector.tensor_reduce(neg_max[:], scores[:], AX.X, ALU.max, negate=True)
         p_sb = sb.tile([P, I], F32, name="p_sb")
@@ -142,10 +151,10 @@ def tile_attend_relayed_excess_counts_kernel(
         inv_sum = sb.tile([P, 1], F32, name="inv_sum")
         nc.vector.reciprocal(inv_sum[:], row_sum[:])
         excess = sb.tile([P, I], F32, name="excess")
-        nc.vector.tensor_scalar(excess[:], p_sb[:], level_sb[:], 0.0, ALU.subtract, ALU.max)
-        ws = sb.tile([P, I], F32, name="ws")
-        nc.vector.tensor_scalar(ws[:], excess[:], inv_sum[:], 256.0, ALU.mult, ALU.mult)
-        nc.vector.tensor_copy(placed[:].indirect(col_list[:]), ws[:])
+        nc.scalar.activation(excess[:], p_sb[:], ACT.Relu, bias=floor_sb[:], scale=256.0)
+        inv_wide = sb.tile([P, I], F32, name="inv_wide")
+        nc.vector.tensor_copy(inv_wide[:], inv_sum[:].to_broadcast([P, I]))
+        nc.vector.tensor_tensor(placed[:].indirect(col_list[:]), excess[:], inv_wide[:], ALU.mult)
 
         c0 = 0
         for k, width in enumerate(OUT_CHUNKS):

@@ -20,6 +20,7 @@ P = 128
 PACK = 4
 LIST_COLS = 32
 N_EARLY = 256
+HUBS_VECTOR = 352
 OUT_CHUNKS = (256, 512, 512, 512, 256)
 
 
@@ -37,22 +38,20 @@ def tile_attend_relayed_excess_counts_kernel(
         hub_rows = [sb.tile([P, U], F32, name="hub_rows%d" % t) for t in range(PACK)]
         q_raw = sb.tile([P, PACK, Q], F32, name="q_raw")
         tie_words = sb.tile([P, T], I32, name="tie_words")
-        tie_bytes = sb.tile([P, T], U8, name="tie_bytes")
-        old_sb = sb.tile([P, M], F32, name="old_sb")
+        tie_bytes = sb.tile([P, T], U8, name="tie_bytes", tag="tie_bytes")
         hf_sb = sb.tile([P, PACK], F32, name="hf_sb")
         level_sb = sb.tile([P, 1], F32, name="level_sb")
         fade_sb = sb.tile([P, 1], F32, name="fade_sb")
         placed = sb.tile([P, M], F32, name="placed")
 
+        got_bytes = sb.tile([P, I], U8, name="got_bytes", align_bytes=64)
         nc.gpsimd.memset(tie_bytes[:].bitcast(I32), 0)
         nc.gpsimd.dma_start(hf_sb[:], hf.rearrange("(p r) o -> p (r o)", r=PACK))
+        nc.gpsimd.memset(got_bytes[:].bitcast(I32), 0)
         nc.gpsimd.memset(placed[:], 0.0)
 
         nc.scalar.dma_start(level_sb[:], level)
-        staged = sb.tile([P, 2, T // 4], I32, name="staged")
-        scale_rows = ties_scales[0].bitcast(I32).rearrange("(h g r) c -> h r g c", h=2, g=2)
-        for h in range(2):
-            nc.scalar.dma_start(staged[64 * h : 64 * h + 4], scale_rows[h])
+        nc.scalar.dma_start(tie_bytes[0:P:8, :].bitcast(I32), ties_scales[0].bitcast(I32))
         hubs_v = hubs.rearrange("(p t) u -> p t u", t=PACK)
         nc.sync.dma_start(hub_list[:], offs2)
         nc.sync.dma_start(hub_rows[0][:], hubs_v[:, 0, :])
@@ -61,60 +60,65 @@ def tile_attend_relayed_excess_counts_kernel(
             nc.sync.dma_start(hub_rows[t][:], hubs_v[:, t, :])
         nc.sync.dma_start(q_raw[:], query.rearrange("(p t) q -> p t q", t=PACK))
         nc.sync.dma_start(tie_words[:], ties_words[0].rearrange("p n t -> p (n t)").bitcast(I32))
+
+        floor_sb = sb.tile([P, 1], F32, name="floor_sb")
+        nc.scalar.activation(floor_sb[:], level_sb[:], ACT.Copy, scale=-256.0)
+
+        picked = sb.tile([P, PACK, J], BF16, name="picked")
+        nc.scalar.activation(picked[:, 0, :], hub_rows[0][:].indirect(hub_list[:]), ACT.Copy)
+
+        got_rows = sb.tile([P, I], U8, name="got_rows")
+        nc.vector.tensor_copy(got_rows[:], tie_bytes[:].indirect(tok_list[:]))
+        for r in range(PACK):
+            nc.sync.dma_start(got_bytes[r:P:32, :].bitcast(I32), got_rows[8 * r : P : 32, :].bitcast(I32))
+        old_sb = sb.tile([P, M], F32, name="old_sb", tag="tie_bytes")
         nc.sync.dma_start(old_sb[:], old)
         nc.sync.dma_start(col_list[:], offs3)
         nc.sync.dma_start(fade_sb[:], fade)
 
-        floor_sb = sb.tile([P, 1], F32, name="floor_sb")
-        nc.scalar.activation(floor_sb[:], level_sb[:], ACT.Copy, scale=-256.0)
-        for g in range(4):
-            lo = 64 * (g // 2)
-            nc.vector.tensor_copy(tie_bytes[32 * g : 32 * g + 4, :].bitcast(I32), staged[lo : lo + 4, g % 2, :])
-
-        picked = sb.tile([P, PACK, J], BF16, name="picked")
-        half = J // 2
-        hc = LIST_COLS // 2
-        got_bytes = sb.tile([P, I], U8, name="got_bytes", align_bytes=64)
-        nc.scalar.activation(picked[:, 0, :], hub_rows[0][:].indirect(hub_list[:]), ACT.Copy)
-        nc.vector.tensor_copy(got_bytes[:], tie_bytes[:].indirect(tok_list[:]))
         nc.scalar.activation(picked[:, 1, :], hub_rows[1][:].indirect(hub_list[:]), ACT.Copy)
-        for t in (2, 3):
-            nc.vector.tensor_copy(picked[:, t, 0:half], hub_rows[t][:].indirect(hub_list[:, 0:hc]))
-            nc.scalar.activation(picked[:, t, half:J], hub_rows[t][:].indirect(hub_list[:, hc:LIST_COLS]), ACT.Copy)
+        for t, nv in ((2, J // 2), (3, HUBS_VECTOR)):
+            nc.vector.tensor_copy(picked[:, t, 0:nv], hub_rows[t][:].indirect(hub_list[:, 0 : nv // 16]))
+            nc.scalar.activation(
+                picked[:, t, nv:J], hub_rows[t][:].indirect(hub_list[:, nv // 16 : LIST_COLS]), ACT.Copy
+            )
 
-        src = picked[:].rearrange("p t (s r) -> p r s t", r=PACK)
-        first_bf = sb.tile([P, 3, P, PACK], BF16, name="first_bf", tag="early", align_bytes=64)
+        woven = sb.tile([P, 1 + PACK, P, PACK], BF16, name="woven", tag="woven", align_bytes=64)
+        src = picked[:].rearrange("p t (s r) -> p s t r", r=PACK)
+        dst = woven[:, 1:].rearrange("p r s t -> p s t r")
+        sv = HUBS_VECTOR // PACK
+        nc.vector.tensor_copy(dst[:, 0:sv], src[:, 0:sv])
+        nc.scalar.copy(dst[:, sv:P], src[:, sv:P])
+        nc.scalar.copy(
+            woven[:, 0].rearrange("p (c i) t -> p c t i", i=PACK),
+            q_raw[:].rearrange("p t (c i) -> p c t i", i=PACK),
+        )
         first_codes = sb.tile([P, 3, P], U32, name="first_codes", align_bytes=64)
         first_scales = sb.tile([P, 3, P], U8, name="first_scales", align_bytes=64)
-        second_bf = sb.tile([P, 2, P, PACK], BF16, name="second_bf", align_bytes=64)
         second_codes = sb.tile([P, 2, P], U32, name="second_codes", tag="late", align_bytes=64)
         second_scales = sb.tile([P, 2, P], U8, name="second_scales", align_bytes=64)
-        nc.scalar.copy(first_bf[:, 2], q_raw[:].rearrange("p t q -> p q t"))
-        nc.vector.tensor_copy(first_bf[:, 0:2], src[:, 0:2])
-        nc.vector.tensor_copy(second_bf[:, 0], src[:, 2])
-        nc.scalar.copy(second_bf[:, 1], src[:, 3])
         hb = ps.tile([P, PACK, Q], F32, name="hb")
-        for h, (bf, codes, scales) in enumerate(
-            ((first_bf, first_codes, first_scales), (second_bf, second_codes, second_scales))
+        for h, (lo, hi, codes, scales) in enumerate(
+            ((0, 3, first_codes, first_scales), (3, 5, second_codes, second_scales))
         ):
             nc.vector.quantize_mx(
                 codes[:].rearrange("p r s -> p (r s)").bitcast(FP8X4),
                 scales[:].rearrange("p r s -> p (r s)"),
-                bf[:].rearrange("p r s t -> p (r s t)"),
+                woven[:, lo:hi].rearrange("p r s t -> p (r s t)"),
             )
             for e in range(2):
                 nc.tensor.matmul_mx(
                     hb[:, 2 * h + e, :],
-                    lhsT=codes[:, e, :].bitcast(FP8X4),
-                    lhsT_scale=scales[:, e, :],
-                    rhs=first_codes[:, 2, :].bitcast(FP8X4),
-                    rhs_scale=first_scales[:, 2, :],
+                    lhsT=codes[:, 1 - h + e, :].bitcast(FP8X4),
+                    lhsT_scale=scales[:, 1 - h + e, :],
+                    rhs=first_codes[:, 0, :].bitcast(FP8X4),
+                    rhs_scale=first_scales[:, 0, :],
                     start=True,
                     stop=True,
                 )
 
         tie_window = tie_words[:].bitcast(U32)
-        words_a = sb.tile([P, N_EARLY], U32, name="words_a", tag="early", align_bytes=64)
+        words_a = sb.tile([P, N_EARLY], U32, name="words_a", tag="woven", align_bytes=64)
         nc.vector.tensor_copy(words_a[:], tie_window.indirect(tok_list[:, 0 : N_EARLY // 16]))
 
         hp_bf = sb.tile([P, Q, PACK], BF16, name="hp_bf", align_bytes=64)
@@ -161,5 +165,5 @@ def tile_attend_relayed_excess_counts_kernel(
             cols = slice(c0, c0 + width)
             res = sb.tile([P, width], F32, name="res%d" % k)
             nc.vector.scalar_tensor_tensor(res[:], old_sb[:, cols], fade_sb[:], placed[:, cols], ALU.mult, ALU.add)
-            nc.sync.dma_start(out[:, cols], res[:])
+            (nc.sync, nc.scalar)[k % 2].dma_start(out[:, cols], res[:])
             c0 = c0 + width

@@ -20,8 +20,8 @@ P = 128
 PACK = 4
 LIST_COLS = 32
 N_EARLY = 256
-HUBS_VECTOR = 352
-OUT_CHUNKS = (256, 512, 512, 512, 256)
+HUBS_VECTOR = 320
+OUT_CHUNKS = (128, 384, 512, 512, 256, 256)
 
 
 def tile_attend_relayed_excess_counts_kernel(
@@ -47,8 +47,8 @@ def tile_attend_relayed_excess_counts_kernel(
         got_bytes = sb.tile([P, I], U8, name="got_bytes", align_bytes=64)
         nc.gpsimd.memset(tie_bytes[:].bitcast(I32), 0)
         nc.gpsimd.dma_start(hf_sb[:], hf.rearrange("(p r) o -> p (r o)", r=PACK))
-        nc.gpsimd.memset(got_bytes[:].bitcast(I32), 0)
-        nc.gpsimd.memset(placed[:], 0.0)
+        nc.vector.memset(got_bytes[:].bitcast(I32), 0)
+        nc.vector.memset(placed[:], 0.0)
 
         nc.scalar.dma_start(level_sb[:], level)
         nc.scalar.dma_start(tie_bytes[0:P:8, :].bitcast(I32), ties_scales[0].bitcast(I32))
@@ -64,9 +64,6 @@ def tile_attend_relayed_excess_counts_kernel(
         floor_sb = sb.tile([P, 1], F32, name="floor_sb")
         nc.scalar.activation(floor_sb[:], level_sb[:], ACT.Copy, scale=-256.0)
 
-        picked = sb.tile([P, PACK, J], BF16, name="picked")
-        nc.scalar.activation(picked[:, 0, :], hub_rows[0][:].indirect(hub_list[:]), ACT.Copy)
-
         got_rows = sb.tile([P, I], U8, name="got_rows")
         nc.vector.tensor_copy(got_rows[:], tie_bytes[:].indirect(tok_list[:]))
         for r in range(PACK):
@@ -76,43 +73,42 @@ def tile_attend_relayed_excess_counts_kernel(
         nc.sync.dma_start(col_list[:], offs3)
         nc.sync.dma_start(fade_sb[:], fade)
 
-        nc.scalar.activation(picked[:, 1, :], hub_rows[1][:].indirect(hub_list[:]), ACT.Copy)
-        for t, nv in ((2, J // 2), (3, HUBS_VECTOR)):
-            nc.vector.tensor_copy(picked[:, t, 0:nv], hub_rows[t][:].indirect(hub_list[:, 0 : nv // 16]))
-            nc.scalar.activation(
-                picked[:, t, nv:J], hub_rows[t][:].indirect(hub_list[:, nv // 16 : LIST_COLS]), ACT.Copy
-            )
-
-        woven = sb.tile([P, 1 + PACK, P, PACK], BF16, name="woven", tag="woven", align_bytes=64)
-        src = picked[:].rearrange("p t (s r) -> p s t r", r=PACK)
-        dst = woven[:, 1:].rearrange("p r s t -> p s t r")
+        woven = sb.tile([P, PACK, P, PACK], BF16, name="woven", tag="woven", align_bytes=64)
+        picked = sb.tile([P, PACK, J - HUBS_VECTOR], BF16, name="picked")
         sv = HUBS_VECTOR // PACK
-        nc.vector.tensor_copy(dst[:, 0:sv], src[:, 0:sv])
-        nc.scalar.copy(dst[:, sv:P], src[:, sv:P])
+        vc = HUBS_VECTOR // 16
+        by_plane = woven[:].rearrange("p r s t -> p t s r")
+        for t in range(PACK):
+            nc.vector.tensor_copy(by_plane[:, t, 0:sv, :], hub_rows[t][:].indirect(hub_list[:, 0:vc]))
+            nc.scalar.activation(picked[:, t, :], hub_rows[t][:].indirect(hub_list[:, vc:LIST_COLS]), ACT.Copy)
         nc.scalar.copy(
-            woven[:, 0].rearrange("p (c i) t -> p c t i", i=PACK),
+            woven[:].rearrange("p r s t -> p s t r")[:, sv:P],
+            picked[:].rearrange("p t (s r) -> p s t r", r=PACK),
+        )
+        q_bf = sb.tile([P, Q, PACK], BF16, name="q_bf", align_bytes=64)
+        q_codes = sb.tile([P, Q], U32, name="q_codes", align_bytes=64)
+        q_scales = sb.tile([P, Q], U8, name="q_scales", align_bytes=64)
+        nc.vector.tensor_copy(
+            q_bf[:].rearrange("p (c i) t -> p c t i", i=PACK),
             q_raw[:].rearrange("p t (c i) -> p c t i", i=PACK),
         )
-        first_codes = sb.tile([P, 3, P], U32, name="first_codes", align_bytes=64)
-        first_scales = sb.tile([P, 3, P], U8, name="first_scales", align_bytes=64)
-        second_codes = sb.tile([P, 2, P], U32, name="second_codes", tag="late", align_bytes=64)
-        second_scales = sb.tile([P, 2, P], U8, name="second_scales", align_bytes=64)
+        nc.vector.quantize_mx(q_codes[:].bitcast(FP8X4), q_scales[:], q_bf[:].rearrange("p q t -> p (q t)"))
         hb = ps.tile([P, PACK, Q], F32, name="hb")
-        for h, (lo, hi, codes, scales) in enumerate(
-            ((0, 3, first_codes, first_scales), (3, 5, second_codes, second_scales))
-        ):
+        for h in range(2):
+            codes = sb.tile([P, 2, P], U32, name="hub_codes%d" % h, tag="hub_codes%d" % h, align_bytes=64)
+            scales = sb.tile([P, 2, P], U8, name="hub_scales%d" % h, align_bytes=64)
             nc.vector.quantize_mx(
                 codes[:].rearrange("p r s -> p (r s)").bitcast(FP8X4),
                 scales[:].rearrange("p r s -> p (r s)"),
-                woven[:, lo:hi].rearrange("p r s t -> p (r s t)"),
+                woven[:, 2 * h : 2 * h + 2].rearrange("p r s t -> p (r s t)"),
             )
             for e in range(2):
                 nc.tensor.matmul_mx(
                     hb[:, 2 * h + e, :],
-                    lhsT=codes[:, 1 - h + e, :].bitcast(FP8X4),
-                    lhsT_scale=scales[:, 1 - h + e, :],
-                    rhs=first_codes[:, 0, :].bitcast(FP8X4),
-                    rhs_scale=first_scales[:, 0, :],
+                    lhsT=codes[:, e, :].bitcast(FP8X4),
+                    lhsT_scale=scales[:, e, :],
+                    rhs=q_codes[:].bitcast(FP8X4),
+                    rhs_scale=q_scales[:],
                     start=True,
                     stop=True,
                 )
@@ -130,7 +126,7 @@ def tile_attend_relayed_excess_counts_kernel(
             ALU.max,
             ALU.mult,
         )
-        words_b = sb.tile([P, I - N_EARLY], U32, name="words_b", tag="late", align_bytes=64)
+        words_b = sb.tile([P, I - N_EARLY], U32, name="words_b", tag="hub_codes1", align_bytes=64)
         nc.vector.tensor_copy(words_b[:], tie_window.indirect(tok_list[:, N_EARLY // 16 : LIST_COLS]))
         hp_codes = sb.tile([P, Q], U32, name="hp_codes", align_bytes=64)
         hp_scales = sb.tile([P, Q], U8, name="hp_scales", align_bytes=64)

from contextlib import ExitStack

import concourse.mybir as mybir

D, T, I, Q, J, U, M = 512, 2048, 512, 128, 512, 1024, 2048
FLOPS = 2 * D * J * Q + 2 * J * Q * I

F32 = mybir.dt.float32
BF16 = mybir.dt.bfloat16
I32 = mybir.dt.int32
U32 = mybir.dt.uint32
U16 = mybir.dt.uint16
U8 = mybir.dt.uint8
FP8X4 = mybir.dt.float8_e4m3fn_x4
ALU = mybir.AluOpType
ACT = mybir.ActivationFunctionType
AX = mybir.AxisListType

P = 128
PACK = 4
LIST_COLS = 32
N_EARLY = 256
HUBS_VECTOR = 320
OUT_CHUNKS = (128, 384, 512, 512, 256, 256)


def tile_attend_relayed_excess_counts_kernel(
    tc, query, hubs, hf, ties_words, ties_scales, level, old, fade, offs, offs2, offs3, out
):
    nc = tc.nc
    with ExitStack() as ctx:
        sb = ctx.enter_context(tc.tile_pool(name="sb", bufs=1))
        ps = ctx.enter_context(tc.psum_pool(name="ps", bufs=1))

        tok_list = sb.tile([P, LIST_COLS], U16, name="tok_list")
        hub_list = sb.tile([P, LIST_COLS], U16, name="hub_list")
        col_list = sb.tile([P, LIST_COLS], U16, name="col_list")
        hub_rows = [sb.tile([P, U], F32, name="hub_rows%d" % t) for t in range(PACK)]
        q_raw = sb.tile([P, PACK, Q], F32, name="q_raw")
        tie_words = sb.tile([P, T], I32, name="tie_words")
        tie_bytes = sb.tile([P, T], U8, name="tie_bytes", tag="tie_bytes")
        hf_sb = sb.tile([P, PACK], F32, name="hf_sb")
        level_sb = sb.tile([P, 1], F32, name="level_sb")
        fade_sb = sb.tile([P, 1], F32, name="fade_sb")
        placed = sb.tile([P, M], F32, name="placed")

        got_bytes = sb.tile([P, I], U8, name="got_bytes", align_bytes=64)
        nc.gpsimd.memset(tie_bytes[:].bitcast(I32), 0)
        nc.gpsimd.dma_start(hf_sb[:], hf.rearrange("(p r) o -> p (r o)", r=PACK))
        nc.vector.memset(got_bytes[:].bitcast(I32), 0)
        nc.vector.memset(placed[:], 0.0)

        nc.scalar.dma_start(level_sb[:], level)
        nc.scalar.dma_start(tie_bytes[0:P:8, :].bitcast(I32), ties_scales[0].bitcast(I32))
        hubs_v = hubs.rearrange("(p t) u -> p t u", t=PACK)
        nc.sync.dma_start(hub_list[:], offs2)
        nc.sync.dma_start(hub_rows[0][:], hubs_v[:, 0, :])
        nc.sync.dma_start(tok_list[:], offs)
        for t in range(1, PACK):
            nc.sync.dma_start(hub_rows[t][:], hubs_v[:, t, :])
        nc.sync.dma_start(q_raw[:], query.rearrange("(p t) q -> p t q", t=PACK))
        nc.sync.dma_start(tie_words[:], ties_words[0].rearrange("p n t -> p (n t)").bitcast(I32))

        floor_sb = sb.tile([P, 1], F32, name="floor_sb")
        nc.scalar.activation(floor_sb[:], level_sb[:], ACT.Copy, scale=-256.0)

        got_rows = sb.tile([P, I], U8, name="got_rows")
        nc.vector.tensor_copy(got_rows[:], tie_bytes[:].indirect(tok_list[:]))
        for r in range(PACK):
            nc.sync.dma_start(got_bytes[r:P:32, :].bitcast(I32), got_rows[8 * r : P : 32, :].bitcast(I32))
        old_sb = sb.tile([P, M], F32, name="old_sb", tag="tie_bytes")
        nc.sync.dma_start(old_sb[:], old)
        nc.sync.dma_start(col_list[:], offs3)
        nc.sync.dma_start(fade_sb[:], fade)

        woven = sb.tile([P, PACK, P, PACK], BF16, name="woven", tag="woven", align_bytes=64)
        picked = sb.tile([P, PACK, J - HUBS_VECTOR], BF16, name="picked")
        sv = HUBS_VECTOR // PACK
        vc = HUBS_VECTOR // 16
        by_plane = woven[:].rearrange("p r s t -> p t s r")
        for t in range(PACK):
            nc.vector.tensor_copy(by_plane[:, t, 0:sv, :], hub_rows[t][:].indirect(hub_list[:, 0:vc]))
            nc.scalar.activation(picked[:, t, :], hub_rows[t][:].indirect(hub_list[:, vc:LIST_COLS]), ACT.Copy)
        nc.scalar.copy(
            woven[:].rearrange("p r s t -> p s t r")[:, sv:P],
            picked[:].rearrange("p t (s r) -> p s t r", r=PACK),
        )
        q_bf = sb.tile([P, Q, PACK], BF16, name="q_bf", align_bytes=64)
        q_codes = sb.tile([P, Q], U32, name="q_codes", align_bytes=64)
        q_scales = sb.tile([P, Q], U8, name="q_scales", align_bytes=64)
        nc.vector.tensor_copy(
            q_bf[:].rearrange("p (c i) t -> p c t i", i=PACK),
            q_raw[:].rearrange("p t (c i) -> p c t i", i=PACK),
        )
        nc.vector.quantize_mx(q_codes[:].bitcast(FP8X4), q_scales[:], q_bf[:].rearrange("p q t -> p (q t)"))
        hb = ps.tile([P, PACK, Q], F32, name="hb")
        for h in range(2):
            codes = sb.tile([P, 2, P], U32, name="hub_codes%d" % h, tag="hub_codes%d" % h, align_bytes=64)
            scales = sb.tile([P, 2, P], U8, name="hub_scales%d" % h, align_bytes=64)
            nc.vector.quantize_mx(
                codes[:].rearrange("p r s -> p (r s)").bitcast(FP8X4),
                scales[:].rearrange("p r s -> p (r s)"),
                woven[:, 2 * h : 2 * h + 2].rearrange("p r s t -> p (r s t)"),
            )
            for e in range(2):
                nc.tensor.matmul_mx(
                    hb[:, 2 * h + e, :],
                    lhsT=codes[:, e, :].bitcast(FP8X4),
                    lhsT_scale=scales[:, e, :],
                    rhs=q_codes[:].bitcast(FP8X4),
                    rhs_scale=q_scales[:],
                    start=True,
                    stop=True,
                )

        tie_window = tie_words[:].bitcast(U32)
        words_a = sb.tile([P, N_EARLY], U32, name="words_a", tag="woven", align_bytes=64)
        nc.vector.tensor_copy(words_a[:], tie_window.indirect(tok_list[:, 0 : N_EARLY // 16]))

        hp_bf = sb.tile([P, Q, PACK], BF16, name="hp_bf", align_bytes=64)
        nc.vector.scalar_tensor_tensor(
            hp_bf[:],
            hb[:].rearrange("p r q -> p q r"),
            0.0,
            hf_sb[:].unsqueeze(1).to_broadcast([P, Q, PACK]),
            ALU.max,
            ALU.mult,
        )
        words_b = sb.tile([P, I - N_EARLY], U32, name="words_b", tag="hub_codes1", align_bytes=64)
        nc.vector.tensor_copy(words_b[:], tie_window.indirect(tok_list[:, N_EARLY // 16 : LIST_COLS]))
        hp_codes = sb.tile([P, Q], U32, name="hp_codes", align_bytes=64)
        hp_scales = sb.tile([P, Q], U8, name="hp_scales", align_bytes=64)
        nc.vector.quantize_mx(hp_codes[:].bitcast(FP8X4), hp_scales[:], hp_bf[:].rearrange("p q r -> p (q r)"))

        scores = ps.tile([P, I], F32, name="scores")
        for words, lo, hi in ((words_a, 0, N_EARLY), (words_b, N_EARLY, I)):
            nc.tensor.matmul_mx(
                scores[:, lo:hi],
                lhsT=hp_codes[:].bitcast(FP8X4),
                lhsT_scale=hp_scales[:],
                rhs=words[:].bitcast(FP8X4),
                rhs_scale=got_bytes[:, lo:hi],
                start=True,
                stop=True,
            )
        neg_max = sb.tile([P, 1], F32, name="neg_max")
        nc.vector.tensor_reduce(neg_max[:], scores[:], AX.X, ALU.max, negate=True)
        p_sb = sb.tile([P, I], F32, name="p_sb")
        row_sum = sb.tile([P, 1], F32, name="row_sum")
        nc.scalar.activation(p_sb[:], scores[:], ACT.Exp, bias=neg_max[:], accum_out=row_sum[:])
        inv_sum = sb.tile([P, 1], F32, name="inv_sum")
        nc.vector.reciprocal(inv_sum[:], row_sum[:])
        excess = sb.tile([P, I], F32, name="excess")
        nc.scalar.activation(excess[:], p_sb[:], ACT.Relu, bias=floor_sb[:], scale=256.0)
        inv_wide = sb.tile([P, I], F32, name="inv_wide")
        nc.vector.tensor_copy(inv_wide[:], inv_sum[:].to_broadcast([P, I]))
        nc.vector.tensor_tensor(placed[:].indirect(col_list[:]), excess[:], inv_wide[:], ALU.mult)

        c0 = 0
        for k, width in enumerate(OUT_CHUNKS):
            cols = slice(c0, c0 + width)
            res = sb.tile([P, width], F32, name="res%d" % k)
            nc.vector.scalar_tensor_tensor(res[:], old_sb[:, cols], fade_sb[:], placed[:, cols], ALU.mult, ALU.add)
            (nc.sync, nc.scalar)[k % 2].dma_start(out[:, cols], res[:])
            c0 = c0 + width
